import numpy as np, ml_dtypes
CORES = [21,29,37,45,53,61,69,77,85]
N = 9
TOK, K = 128, 2
EPS = 0.01
ROUTE = [[[7,8],[2,4],[0,4],[2,8],[0,4],[2,8],[7,8],[0,3],[3,8],[0,4],[3,5],[1,8],[6,7],[0,7],[1,6],[7,8],[1,2],[4,6],[3,6],[4,8],[1,3],[6,7],[0,3],[4,8],[2,8],[3,8],[0,3],[4,6],[2,6],[3,8],[5,8],[7,8],[3,8],[0,5],[2,8],[1,3],[2,4],[1,5],[2,8],[4,6],[0,1],[0,8],[2,6],[6,7],[1,7],[0,7],[0,7],[2,5],[6,7],[1,2],[3,6],[0,3],[0,2],[0,4],[1,3],[0,5],[2,6],[1,5],[2,5],[0,2],[2,4],[2,5],[2,4],[2,8],[3,6],[1,7],[0,1],[3,7],[1,2],[3,4],[1,2],[3,5],[2,5],[0,5],[2,7],[1,2],[2,3],[0,3],[7,8],[3,4],[3,5],[0,6],[4,5],[3,7],[1,3],[0,4],[5,6],[2,7],[4,7],[0,4],[5,6],[3,7],[5,6],[0,1],[2,7],[4,7],[7,8],[1,4],[1,7],[2,3],[2,8],[3,6],[2,5],[0,7],[2,8],[3,8],[5,8],[0,4],[5,6],[1,2],[3,7],[3,8],[0,5],[0,1],[2,6],[0,7],[0,5],[0,8],[1,5],[7,8],[0,4],[0,2],[0,2],[0,4],[2,4],[5,7],[3,8],[3,7]],[[0,1],[5,7],[0,5],[4,8],[0,1],[3,5],[3,7],[1,7],[1,8],[3,7],[0,3],[5,7],[6,7],[0,6],[6,7],[1,3],[1,3],[0,7],[6,8],[0,7],[1,4],[3,7],[1,5],[1,8],[1,6],[4,8],[1,8],[6,8],[0,3],[1,5],[6,8],[1,4],[5,7],[4,8],[2,4],[2,7],[2,7],[0,8],[4,6],[3,7],[1,4],[2,8],[1,8],[2,6],[3,7],[4,7],[4,5],[3,7],[0,2],[0,2],[4,5],[0,6],[3,5],[0,8],[0,6],[5,7],[1,4],[2,6],[1,8],[0,8],[4,7],[1,7],[3,7],[4,6],[2,8],[1,4],[1,3],[2,7],[0,2],[0,3],[2,5],[0,6],[5,8],[5,8],[0,5],[0,4],[4,7],[1,5],[5,7],[0,7],[2,7],[2,3],[0,7],[1,7],[4,8],[3,4],[4,6],[5,8],[2,3],[0,3],[5,7],[0,4],[1,6],[0,1],[2,8],[3,6],[0,8],[1,7],[0,8],[1,6],[4,5],[0,7],[0,8],[1,4],[2,4],[0,7],[0,5],[5,7],[3,4],[0,4],[5,7],[1,5],[1,6],[3,5],[2,7],[5,7],[5,6],[0,8],[1,4],[0,5],[4,8],[0,4],[2,6],[4,7],[1,5],[0,1],[2,8],[4,6]],[[5,8],[2,8],[1,6],[5,6],[5,8],[5,7],[5,7],[1,8],[3,5],[3,7],[5,8],[2,4],[1,3],[1,5],[0,1],[1,4],[0,3],[0,2],[4,7],[2,6],[1,2],[2,8],[0,8],[6,7],[4,6],[2,8],[2,6],[3,7],[3,5],[5,8],[0,6],[6,8],[4,8],[5,8],[0,7],[3,5],[0,3],[0,6],[3,5],[1,2],[0,7],[7,8],[4,8],[3,4],[0,2],[3,7],[1,5],[7,8],[2,3],[7,8],[1,7],[0,6],[1,6],[5,8],[2,5],[3,6],[5,8],[4,8],[5,7],[5,6],[2,8],[0,1],[3,7],[6,8],[1,6],[3,8],[5,6],[4,5],[1,4],[1,6],[3,4],[4,8],[2,8],[1,6],[0,4],[0,8],[1,2],[1,5],[1,4],[3,7],[1,8],[3,7],[3,7],[0,6],[1,7],[6,8],[2,5],[5,8],[0,7],[0,6],[5,7],[1,5],[2,6],[0,2],[3,8],[1,6],[0,5],[5,7],[1,3],[3,5],[0,1],[0,4],[0,2],[2,5],[2,3],[2,8],[3,5],[2,7],[1,3],[2,3],[4,5],[0,2],[1,6],[0,5],[0,6],[4,6],[0,3],[2,8],[2,8],[3,7],[3,4],[0,4],[3,4],[1,5],[2,3],[3,8],[3,7],[1,7]],[[1,8],[4,7],[2,6],[1,5],[1,6],[3,7],[3,6],[0,5],[0,3],[0,4],[0,8],[1,5],[6,7],[2,6],[1,5],[0,3],[2,4],[0,5],[2,4],[3,8],[0,2],[4,6],[2,8],[0,1],[2,3],[4,6],[0,8],[0,1],[0,7],[0,6],[3,5],[3,7],[3,4],[4,8],[0,3],[5,7],[3,7],[1,2],[4,5],[0,4],[2,5],[1,7],[2,4],[2,6],[0,8],[2,7],[1,4],[3,8],[2,4],[3,5],[4,8],[1,3],[1,3],[0,1],[5,6],[1,5],[0,3],[4,5],[4,5],[0,1],[4,8],[2,4],[3,7],[3,6],[2,8],[5,6],[6,8],[2,5],[1,7],[5,8],[4,8],[0,6],[3,8],[1,6],[0,7],[1,3],[1,3],[2,3],[0,8],[5,7],[6,7],[1,8],[1,7],[1,8],[0,8],[0,2],[4,7],[6,8],[4,8],[3,4],[2,4],[2,7],[1,4],[3,8],[6,7],[7,8],[1,2],[3,6],[0,2],[4,7],[1,2],[0,3],[2,6],[5,8],[2,4],[4,8],[5,7],[4,7],[6,8],[1,5],[1,4],[2,6],[4,8],[4,7],[2,3],[2,3],[3,5],[6,8],[0,5],[0,2],[1,2],[0,6],[2,5],[4,7],[6,8],[0,3],[3,5],[2,8]],[[5,7],[4,7],[6,8],[0,3],[4,5],[2,5],[5,7],[2,7],[5,7],[2,3],[1,6],[0,6],[2,6],[1,2],[2,7],[3,7],[0,3],[2,4],[3,7],[0,8],[2,3],[0,5],[5,6],[0,4],[0,3],[0,4],[4,6],[2,8],[4,8],[6,7],[3,4],[2,6],[5,7],[0,4],[6,8],[5,6],[0,2],[1,6],[2,7],[1,2],[3,8],[3,6],[0,4],[2,8],[7,8],[6,7],[4,5],[0,3],[0,7],[5,6],[4,5],[6,7],[1,3],[1,8],[2,4],[3,7],[2,4],[3,8],[4,7],[0,2],[6,8],[2,7],[0,1],[5,7],[0,7],[0,2],[1,6],[6,7],[0,3],[1,7],[2,8],[0,3],[0,2],[2,8],[1,5],[0,3],[5,8],[3,5],[1,3],[1,6],[4,5],[5,7],[2,5],[4,7],[6,7],[0,5],[2,3],[1,6],[1,5],[4,8],[2,5],[3,6],[3,6],[2,8],[3,8],[3,7],[0,5],[6,8],[1,7],[1,2],[4,5],[1,6],[0,8],[2,4],[6,8],[1,3],[0,1],[4,8],[0,2],[1,7],[0,7],[3,7],[4,5],[0,4],[5,6],[1,2],[0,2],[4,8],[5,7],[4,7],[1,2],[3,4],[4,8],[0,3],[1,8],[7,8],[2,5],[4,6]],[[1,3],[5,6],[4,5],[0,2],[5,8],[0,1],[1,2],[2,5],[3,7],[5,6],[1,8],[1,8],[4,7],[2,5],[4,5],[1,8],[3,6],[0,1],[0,2],[5,8],[5,7],[4,5],[4,7],[2,3],[5,7],[1,3],[0,3],[3,5],[3,8],[5,6],[0,7],[6,7],[0,7],[4,5],[2,3],[3,5],[0,6],[4,6],[1,5],[2,5],[3,8],[3,7],[0,5],[0,1],[0,6],[1,8],[1,5],[0,6],[5,6],[4,7],[0,5],[1,4],[2,7],[0,4],[0,4],[3,8],[2,5],[1,7],[3,5],[0,5],[3,6],[0,1],[1,5],[0,2],[3,4],[1,7],[2,8],[6,8],[2,5],[0,7],[3,4],[4,7],[2,6],[6,8],[5,8],[2,4],[0,4],[1,2],[1,8],[1,4],[2,5],[7,8],[6,7],[0,5],[0,1],[1,2],[1,3],[0,2],[4,7],[3,4],[4,8],[1,5],[1,2],[4,6],[0,8],[3,8],[0,7],[6,7],[0,4],[3,7],[5,6],[3,5],[0,3],[0,5],[0,8],[4,6],[1,3],[0,6],[1,4],[0,2],[3,7],[0,5],[3,6],[5,8],[7,8],[1,5],[1,6],[1,5],[3,5],[0,8],[2,3],[1,3],[4,6],[0,5],[1,5],[0,1],[5,6],[2,7]],[[1,2],[5,6],[0,6],[0,7],[2,5],[2,7],[4,7],[0,2],[3,6],[5,6],[1,7],[1,6],[2,3],[0,2],[0,8],[5,7],[0,8],[0,3],[2,4],[2,3],[4,8],[1,8],[0,4],[7,8],[5,6],[1,5],[0,6],[2,7],[4,7],[5,7],[2,4],[1,8],[1,6],[1,6],[3,5],[2,3],[1,5],[5,7],[2,3],[2,7],[0,2],[3,5],[3,6],[5,8],[3,5],[1,8],[2,4],[2,5],[0,7],[1,8],[3,7],[3,7],[6,8],[7,8],[4,8],[1,5],[2,5],[5,8],[2,7],[6,8],[6,8],[0,1],[2,7],[2,8],[4,5],[5,7],[4,5],[0,1],[2,6],[1,4],[6,7],[2,5],[6,8],[6,8],[1,8],[1,5],[4,6],[0,5],[4,6],[0,5],[4,8],[3,5],[2,4],[2,3],[2,7],[0,5],[3,7],[0,5],[4,7],[2,3],[2,6],[2,3],[2,3],[0,3],[4,5],[1,6],[1,4],[5,8],[0,4],[1,6],[0,3],[3,6],[1,8],[4,7],[4,7],[1,3],[3,5],[4,7],[1,2],[1,3],[0,2],[6,7],[0,3],[5,7],[5,7],[0,5],[6,7],[1,3],[4,5],[0,2],[4,6],[2,8],[4,5],[0,7],[1,5],[2,7],[0,1],[2,5]],[[0,1],[5,8],[0,6],[2,7],[4,5],[3,8],[1,3],[1,4],[1,3],[1,5],[4,6],[0,2],[3,7],[0,3],[6,7],[3,6],[3,5],[0,3],[2,6],[0,3],[0,7],[7,8],[2,3],[4,5],[0,1],[5,7],[4,5],[0,8],[0,6],[4,8],[0,3],[3,5],[0,4],[1,6],[3,4],[1,3],[4,8],[3,5],[2,8],[1,5],[3,6],[7,8],[7,8],[0,4],[3,6],[5,8],[4,8],[2,8],[1,6],[2,4],[0,2],[0,7],[0,3],[5,7],[4,5],[1,4],[4,5],[5,8],[0,3],[0,7],[4,8],[1,7],[3,5],[2,8],[3,7],[2,6],[1,4],[0,3],[2,6],[4,5],[1,5],[2,6],[1,7],[3,8],[6,7],[2,7],[3,4],[0,6],[1,2],[0,2],[4,5],[5,8],[0,5],[1,2],[6,7],[3,6],[1,3],[0,4],[3,7],[5,8],[0,3],[2,7],[0,7],[6,8],[4,6],[0,2],[0,7],[7,8],[4,5],[5,8],[5,7],[3,5],[3,5],[2,3],[0,3],[6,8],[1,4],[1,3],[2,3],[0,8],[6,7],[2,6],[0,1],[1,2],[4,7],[1,5],[7,8],[3,5],[3,5],[1,7],[3,6],[2,6],[3,6],[2,6],[2,5],[4,6],[2,3],[0,4]],[[1,3],[0,5],[0,4],[0,3],[1,5],[6,7],[3,8],[3,6],[1,5],[5,6],[4,6],[0,4],[3,8],[2,8],[0,5],[3,5],[0,6],[0,2],[2,3],[0,8],[1,7],[1,4],[3,5],[7,8],[0,1],[1,8],[6,7],[2,7],[4,8],[3,5],[4,7],[4,6],[3,8],[3,6],[4,5],[6,8],[0,4],[1,5],[3,6],[5,8],[0,6],[3,5],[1,5],[1,2],[4,8],[0,1],[7,8],[3,5],[1,5],[3,6],[1,8],[3,7],[0,5],[0,2],[7,8],[2,6],[1,2],[4,7],[1,6],[3,8],[1,5],[4,8],[0,6],[3,7],[1,3],[1,7],[2,8],[0,4],[7,8],[0,8],[2,8],[0,4],[1,8],[2,3],[0,7],[2,3],[0,2],[7,8],[1,2],[6,7],[5,8],[0,8],[4,5],[0,7],[3,8],[0,7],[2,3],[0,4],[1,6],[1,2],[1,2],[5,7],[3,6],[5,8],[3,6],[2,8],[4,6],[1,7],[2,4],[1,5],[1,5],[4,5],[1,5],[2,5],[4,8],[7,8],[0,8],[1,4],[1,2],[4,8],[2,8],[2,7],[4,6],[1,3],[1,7],[0,4],[4,6],[0,5],[6,8],[4,8],[4,6],[3,5],[0,5],[6,8],[1,3],[2,7],[5,7],[1,8]]]
def sigmoid(z):
    a = np.exp(-np.abs(z)); return np.where(z >= 0, 1.0, a) / (1.0 + a)
def setup_inputs(rng):
    rt = (0.75 * rng.standard_normal((128, 1), dtype=np.float32) + rng.standard_normal((128, N), dtype=np.float32) / 2).astype(ml_dtypes.bfloat16)
    rm = np.zeros((N, N, TOK), np.float32)
    for r in range(N):
        for t in range(TOK): rm[r, ROUTE[r][t], t] = 1.0
    return {"x": (rng.standard_normal((N, 128, TOK), dtype=np.float32) / 8).astype(ml_dtypes.bfloat16), "rt": np.broadcast_to(rt, (N, 128, N)).copy(), "rm": rm.astype(ml_dtypes.bfloat16), "w": rng.standard_normal((N, 128, 128), dtype=np.float32).astype(ml_dtypes.bfloat16)}
def setup_inputs_big(rng):
    d = setup_inputs(rng)
    for k in ("x", "w"): d[k] = (d[k].astype(np.float32) * 1024.0).astype(d[k].dtype)
    return d
def setup_inputs_small(rng):
    d = setup_inputs(rng)
    for k in ("x", "w"): d[k] = (d[k].astype(np.float32) * (1 / 1024.0)).astype(d[k].dtype)
    return d
def setup_inputs_apart(rng):
    d = setup_inputs(rng)
    f = (10.0 ** rng.permutation(np.linspace(-1.5, 1.5, N))).astype(np.float32).reshape(N, 1, 1)
    for k in ("x",): d[k] = (d[k].astype(np.float32) * f).astype(d[k].dtype)
    return d
def setup_inputs_faint(rng):
    d = setup_inputs(rng); x = d["x"].astype(np.float32); rt = d["rt"][0].astype(np.float32); t = int(rng.integers(N))
    p = rt @ np.linalg.solve(rt.T @ rt, np.ones(N, np.float32))
    x[t] = x[t] / 16 - np.outer(p, rng.uniform(20, 22, TOK).astype(np.float32))
    d["x"] = x.astype(d["x"].dtype)
    return d
def reference(x, rt, rm, w):
    X, RT, W = x.astype(np.float64), rt.astype(np.float64), w.astype(np.float64)
    y = np.zeros((N, 128, TOK))
    for r in range(N):
        sc = RT[r].T @ X[r]
        for t in range(TOK):
            ex = ROUTE[r][t]; g = sigmoid(sc[ex, t]); g = g / (g.sum() + EPS)
            y[r][:, t] = sum(g[i] * (W[e].T @ X[r][:, t]) for i, e in enumerate(ex))
    return {"y": y.astype(ml_dtypes.bfloat16)}

@@ -1,0 +1,223 @@
+from concourse.bass import DstId, RemoteDMATransfer
+from concourse.mybir import AluOpType, ActivationFunctionType
+
+N = 9
+D = 128
+EPS = 0.01
+SIM_CORES = 96
+GROUP = 2
+NB = (N + GROUP - 1) // GROUP
+
+SCRATCH = {
+    "wsrc": ("dram", [128, D], "bfloat16"),
+    "relay": ("dram", [128, D], "bfloat16"),
+    "wall": ("sbuf", [128, N * D], "bfloat16"),
+    "xs": ("sbuf", [128, D], "bfloat16"),
+    "rts": ("sbuf", [128, 16], "bfloat16"),
+    "rms": ("sbuf", [128, D], "bfloat16"),
+    "cmp": ("sbuf", [128, 16], "float32"),
+    "i9": ("sbuf", [128, 16], "float32"),
+    "ones": ("sbuf", [128, D], "bfloat16"),
+    "sel": ("sbuf", [128, N * D], "bfloat16"),
+    "am": ("sbuf", [128, D], "bfloat16"),
+    "xg": ("sbuf", [128, N * D], "bfloat16"),
+    "r0": ("sbuf", [128, D], "float32"),
+    "rr": ("sbuf", [128, D], "float32"),
+    "ysb": ("sbuf", [128, D], "bfloat16"),
+    "ps_sc": ("psum", [128, 512], "float32"),
+    "ps_acc": ("psum", [128, 512], "float32"),
+}
+for _j in range(NB):
+    SCRATCH["pb%d" % _j] = ("psum", [128, 512], "float32")
+
+SEMAPHORES = (["wd", "wo", "xr", "rm", "cm", "pre", "sel", "sc", "a", "am", "den", "r0", "rr", "mm", "y", "st", "loc"]
+              + ["b%d" % j for j in range(NB)] + ["x%d" % j for j in range(NB)] + ["a%d" % s for s in range(N)])
+
+
+def _count(mask):
+    return bin(mask).count("1")
+
+
+def _common_mask(topo, src, dsts):
+    m = topo.mask(src, dsts[0])
+    for d in dsts[1:]:
+        m &= topo.mask(src, d)
+    return m
+
+
+def _plan(T, topo):
+    cores = list(T.cores)
+    n = len(cores)
+    chips_used = [topo.chip(c) for c in cores]
+    first, away, role = {}, {}, {}
+    when = {r: {} for r in range(n)}
+    by = {r: {} for r in range(n)}
+    taken = []
+    for s, c in enumerate(cores):
+        ring = [(s + k) % n for k in range(1, n)]
+        direct = [d for d in ring if topo.may_write(c, cores[d])]
+        cross = [d for d in ring if not topo.may_write(c, cores[d])]
+        away[s] = []
+        rest = []
+        for d in cross:
+            spare = [h for h in range(SIM_CORES)
+                     if topo.mates(topo.chip(h), topo.chip(cores[d])) and topo.chip(h) not in chips_used
+                     and topo.may_write(c, h) and topo.may_write(h, cores[d]) and h not in taken]
+            if spare:
+                dies = [topo.die(h) for h in taken if topo.chip(h) == topo.chip(spare[0])]
+                spare.sort(key=lambda h: (dies.count(topo.die(h)), h))
+                h = spare[0]
+                taken.append(h)
+                role[h] = (s, [d])
+                away[s].append((h, True))
+                when[d][s] = 3.4
+                by[d][s] = h
+            else:
+                rest.append(d)
+        for d in direct:
+            away[s].append((cores[d], False))
+            when[d][s] = float(len(away[s]))
+            by[d][s] = c
+        owners = [h for h in range(SIM_CORES) if topo.chip(h) == topo.chip(c) and h not in cores
+                  and all(topo.may_write(h, cores[d]) for d in rest)]
+        near = [h for h in owners if topo.die(h) == topo.die(c)]
+        far = [h for h in owners if topo.die(h) != topo.die(c)]
+        mate = [d for d in rest if topo.mates(topo.chip(c), topo.chip(cores[d]))]
+        two = [d for d in rest if d not in mate]
+        if not mate:
+            mate = [two.pop()]
+        jobs = {h: [] for h in far}
+        for k, d in enumerate(two):
+            jobs[far[k % len(far)]].append(d)
+            when[d][s] = 3.5 + k // len(far)
+        jobs[near[0]] = mate
+        when[mate[0]][s] = 3.2
+        first[s] = [h for h in far + near[:1] if jobs[h]]
+        for h in first[s]:
+            role[h] = (s, jobs[h])
+            for d in jobs[h]:
+                by[d][s] = h
+    return first, away, role, when, by
+
+
+def _slot(T, e):
+    return T.wall[:, e * D:(e + 1) * D]
+
+
+def _send(g, T, topo, mask, src, dst_cores, dst_aps, sem):
+    ids = []
+    for d in dst_cores:
+        rid, pid, _se = topo.addr(d)
+        ids.append(DstId(rid=rid, pnc=pid))
+    g.remote_dma_fused([RemoteDMATransfer(dst_ids=ids, dma_engine_mask=mask, remote_sem=sem, srcs=[src],
+                                          dsts=dst_aps, alu_op=0)], local_sem=T.sem.loc)
+
+
+def _masks(T, topo, s, first, away):
+    c = T.cores[s]
+    m_off = _common_mask(topo, c, [h for h, _r in away[s]])
+    m_on = _common_mask(topo, c, first[s])
+    if m_on & ~m_off:
+        m_on &= ~m_off
+    return m_on, m_off
+
+
+def _relay_program(g, core, T, topo, plan):
+    first, away, role, when, by = plan
+    s, dests = role[core]
+    m_on, m_off = _masks(T, topo, s, first, away)
+    sem = T.sem["a%d" % s]
+    g.wait_ge(sem, _count(m_on if core in first[s] else m_off))
+    dst = [T.cores[d] for d in dests]
+    mask = _common_mask(topo, core, dst)
+    _send(g, T, topo, mask, T.relay[:, :], dst, [_slot(T, s) for _d in dests], sem)
+    g.wait_ge(T.sem.loc, _count(mask))
+
+
+def _rank_program(g, core, T, topo, plan):
+    first, away, role, when, by = plan
+    r = T.rank_of(core)
+    S = T.sem
+    v, t, sc, sy = g.vector, g.tensor, g.scalar, g.sync
+    mult = AluOpType.mult
+    order = [r] + sorted(when[r], key=lambda s: (when[r][s], s))
+    groups = [list(range(j * GROUP, min(N, (j + 1) * GROUP))) for j in range(NB)]
+
+    def blk(buf, i):
+        return buf[:, i * D:(i + 1) * D]
+
+    sy.dma_start(T.wsrc[:, :], T.w[:, :]).then_inc(S.wd, 16)
+    sc.dma_start(T.xs[:, :], T.x[:, :]).then_inc(S.xr, 16)
+    sy.dma_start(T.rts[:, 0:N], T.rt[:, :]).then_inc(S.xr, 16)
+    sc.dma_start(T.rms[0:N, :], T.rm[:, :]).then_inc(S.rm, 16)
+    sy.dma_start(_slot(T, r), T.w[:, :]).then_inc(S.wo, 16)
+
+    g.iota(T.cmp[0:N, 0:N], [[1, N]], 0, -1, allow_small_or_imprecise_dtypes=True).then_inc(S.cm, 1)
+    m_on, m_off = _masks(T, topo, r, first, away)
+    g.wait_ge(S.wd, 16)
+    mine = S["a%d" % r]
+    _send(g, T, topo, m_on, T.wsrc[:, :], first[r], [T.relay[:, :] for _h in first[r]], mine)
+    _send(g, T, topo, m_off, T.wsrc[:, :], [h for h, _x in away[r]],
+          [T.relay[:, :] if x else _slot(T, r) for _h, x in away[r]], mine)
+    g.wait_ge(S.loc, _count(m_on) + _count(m_off))
+
+    v.memset(T.ones[0:N, :], 1.0).then_inc(S.pre, 1)
+    v.wait_ge(S.cm, 1)
+    v.tensor_scalar(T.i9[0:N, 0:N], T.cmp[0:N, 0:N], 0.0, None, AluOpType.is_equal).then_inc(S.pre, 1)
+    v.wait_ge(S.pre, 2)
+    for i, e in enumerate(order):
+        v.tensor_scalar(T.sel[0:N, i * D:(i + 1) * D], T.ones[0:N, :], T.i9[0:N, e:e + 1], None, mult).then_inc(S.sel, 1)
+
+    t.wait_ge(S.xr, 32)
+    t.matmul(T.ps_sc[0:N, 0:D], T.rts[:, 0:N], T.xs[:, :], True, True).then_inc(S.sc, 1)
+    sc.wait_ge(S.sc, 1)
+    sc.activation(T.ps_sc[0:N, D:2 * D], T.ps_sc[0:N, 0:D], ActivationFunctionType.Sigmoid).then_inc(S.a, 1)
+    v.wait_ge(S.a, 1)
+    v.wait_ge(S.rm, 16)
+    v.tensor_tensor(T.am[0:N, :], T.ps_sc[0:N, D:2 * D], T.rms[0:N, :], mult).then_inc(S.am, 1)
+
+    t.wait_ge(S.pre, 2)
+    t.wait_ge(S.sel, N)
+    t.wait_ge(S.am, 1)
+    v.wait_ge(S.xr, 32)
+    for j, grp in enumerate(groups):
+        for i in grp:
+            t.matmul(blk(T["pb%d" % j], i - grp[0]), T.sel[0:N, i * D:(i + 1) * D], T.am[0:N, :], True, True) \
+                .then_inc(S["b%d" % j], 1)
+        v.wait_ge(S["b%d" % j], len(grp))
+        for i in grp:
+            v.tensor_tensor(blk(T.xg, i), blk(T["pb%d" % j], i - grp[0]), T.xs[:, :], mult).then_inc(S["x%d" % j], 1)
+    t.matmul(T.ps_sc[:, 2 * D:3 * D], T.ones[0:N, :], T.am[0:N, :], True, True).then_inc(S.den, 1)
+    sc.wait_ge(S.den, 1)
+    sc.activation(T.r0[:, :], T.ps_sc[:, 2 * D:3 * D], ActivationFunctionType.Identity, bias=EPS).then_inc(S.r0, 1)
+    v.wait_ge(S.r0, 1)
+    v.reciprocal(T.rr[:, :], T.r0[:, :]).then_inc(S.rr, 1)
+
+    for i, e in enumerate(order):
+        if i % GROUP == 0:
+            t.wait_ge(S["x%d" % (i // GROUP)], len(groups[i // GROUP]))
+        if e == r:
+            t.wait_ge(S.wo, 16)
+        else:
+            h = by[r][e]
+            if h == T.cores[e]:
+                cnt = _count(_masks(T, topo, e, first, away)[1])
+            else:
+                cnt = _count(_common_mask(topo, h, [T.cores[d] for d in role[h][1]]))
+            t.wait_ge(S["a%d" % e], cnt)
+        t.matmul(T.ps_acc[:, 0:D], _slot(T, e), blk(T.xg, i), i == 0, i == N - 1).then_inc(S.mm, 1)
+
+    v.wait_ge(S.rr, 1)
+    v.wait_ge(S.mm, N)
+    v.tensor_tensor(T.ysb[:, :], T.ps_acc[:, 0:D], T.rr[:, :], mult).then_inc(S.y, 1)
+    sy.wait_ge(S.y, 1)
+    sy.dma_start(T.y[:, :], T.ysb[:, :]).then_inc(S.st, 16)
+    sy.wait_ge(S.st, 16)
+
+
+def rank_program(g, core, T, topo):
+    plan = _plan(T, topo)
+    if T.rank_of(core) is not None:
+        _rank_program(g, core, T, topo, plan)
+    elif core in plan[2]:
+        _relay_program(g, core, T, topo, plan)

@@ -15,13 +15,15 @@ SCRATCH = {
     "xs": ("sbuf", [128, D], "bfloat16"),
     "rts": ("sbuf", [128, 16], "bfloat16"),
     "rms": ("sbuf", [128, D], "bfloat16"),
-    "cmp": ("sbuf", [128, 16], "float32"),
-    "i9": ("sbuf", [128, 16], "float32"),
+    "cmp": ("sbuf", [128, D], "float32"),
+    "eye": ("sbuf", [128, D], "bfloat16"),
     "ones": ("sbuf", [128, D], "bfloat16"),
     "sel": ("sbuf", [128, N * D], "bfloat16"),
     "am": ("sbuf", [128, D], "bfloat16"),
     "xg": ("sbuf", [128, N * D], "bfloat16"),
-    "r0": ("sbuf", [128, D], "float32"),
+    "dn": ("sbuf", [128, 4], "float32"),
+    "rd": ("sbuf", [128, 4], "float32"),
+    "dg": ("sbuf", [128, D], "bfloat16"),
     "rr": ("sbuf", [128, D], "float32"),
     "ysb": ("sbuf", [128, D], "bfloat16"),
     "ps_sc": ("psum", [128, 512], "float32"),
@@ -30,7 +32,8 @@ SCRATCH = {
 for _j in range(NB):
     SCRATCH["pb%d" % _j] = ("psum", [128, 512], "float32")
 
-SEMAPHORES = (["wd", "wo", "xr", "rm", "cm", "pre", "sel", "sc", "a", "am", "den", "r0", "rr", "mm", "y", "st", "loc"]
+SEMAPHORES = (["wd", "wo", "xr", "rm", "cm", "pre", "sel", "sc", "a", "am", "dt", "dn", "rd", "dg", "rp", "rr", "mm",
+               "y", "st", "loc"]
               + ["b%d" % j for j in range(NB)] + ["x%d" % j for j in range(NB)] + ["a%d" % s for s in range(N)])
 
 
@@ -48,94 +51,78 @@ def _common_mask(topo, src, dsts):
 def _plan(T, topo):
     cores = list(T.cores)
     n = len(cores)
-    chips_used = [topo.chip(c) for c in cores]
-    first, away, role = {}, {}, {}
+    hi, lo, plain, role = {}, {}, {}, {}
     when = {r: {} for r in range(n)}
     by = {r: {} for r in range(n)}
-    taken = []
+    met = {}
     for s, c in enumerate(cores):
         ring = [(s + k) % n for k in range(1, n)]
-        direct = [d for d in ring if topo.may_write(c, cores[d])]
+        plain[s] = [d for d in ring if topo.may_write(c, cores[d])]
         cross = [d for d in ring if not topo.may_write(c, cores[d])]
-        away[s] = []
-        rest = []
-        for d in cross:
-            spare = [h for h in range(SIM_CORES)
-                     if topo.mates(topo.chip(h), topo.chip(cores[d])) and topo.chip(h) not in chips_used
-                     and topo.may_write(c, h) and topo.may_write(h, cores[d]) and h not in taken]
-            if spare:
-                dies = [topo.die(h) for h in taken if topo.chip(h) == topo.chip(spare[0])]
-                spare.sort(key=lambda h: (dies.count(topo.die(h)), h))
-                h = spare[0]
-                taken.append(h)
-                role[h] = (s, [d])
-                away[s].append((h, True))
-                when[d][s] = 3.4
-                by[d][s] = h
-            else:
-                rest.append(d)
-        for d in direct:
-            away[s].append((cores[d], False))
-            when[d][s] = float(len(away[s]))
-            by[d][s] = c
         owners = [h for h in range(SIM_CORES) if topo.chip(h) == topo.chip(c) and h not in cores
-                  and all(topo.may_write(h, cores[d]) for d in rest)]
+                  and all(topo.may_write(h, cores[d]) for d in cross)]
         near = [h for h in owners if topo.die(h) == topo.die(c)]
         far = [h for h in owners if topo.die(h) != topo.die(c)]
-        mate = [d for d in rest if topo.mates(topo.chip(c), topo.chip(cores[d]))]
-        two = [d for d in rest if d not in mate]
-        if not mate:
-            mate = [two.pop()]
-        jobs = {h: [] for h in far}
-        for k, d in enumerate(two):
-            jobs[far[k % len(far)]].append(d)
-            when[d][s] = 3.5 + k // len(far)
-        jobs[near[0]] = mate
-        when[mate[0]][s] = 3.2
-        first[s] = [h for h in far + near[:1] if jobs[h]]
-        for h in first[s]:
+        mate = [d for d in cross if topo.mates(topo.chip(c), topo.chip(cores[d]))]
+        two = [d for d in cross if d not in mate]
+        dn, df = topo.die(near[0]), topo.die(far[0])
+        two.sort(key=lambda d: (met.get((d, dn), 0) - met.get((d, df), 0), ring.index(d)))
+        k = len(two) - len(far)
+        jobs = {h: [] for h in owners}
+        for h, d in zip(far, two[k:]):
+            jobs[h].append(d)
+            met[(d, df)] = met.get((d, df), 0) + 1
+        for i, d in enumerate(two[:k]):
+            jobs[near[::-1][i % len(near)]].append(d)
+            met[(d, dn)] = met.get((d, dn), 0) + 1
+        jobs[near[0]] += mate
+        hi[s] = [h for h in far if jobs[h]]
+        lo[s] = [h for h in near[::-1] if jobs[h]]
+        for h in hi[s] + lo[s]:
             role[h] = (s, jobs[h])
-            for d in jobs[h]:
+            for i, d in enumerate(jobs[h]):
+                when[d][s] = 3.0 + i
                 by[d][s] = h
-    return first, away, role, when, by
+        for i, d in enumerate(plain[s]):
+            when[d][s] = 1.0 + 0.1 * i
+            by[d][s] = c
+    return hi, lo, plain, role, when, by
 
 
 def _slot(T, e):
     return T.wall[:, e * D:(e + 1) * D]
 
 
-def _send(g, T, topo, mask, src, dst_cores, dst_aps, sem):
+def _transfer(topo, mask, src, dst_cores, dst_aps, sem):
     ids = []
     for d in dst_cores:
         rid, pid, _se = topo.addr(d)
         ids.append(DstId(rid=rid, pnc=pid))
-    g.remote_dma_fused([RemoteDMATransfer(dst_ids=ids, dma_engine_mask=mask, remote_sem=sem, srcs=[src],
-                                          dsts=dst_aps, alu_op=0)], local_sem=T.sem.loc)
+    return RemoteDMATransfer(dst_ids=ids, dma_engine_mask=mask, remote_sem=sem, srcs=[src], dsts=dst_aps, alu_op=0)
 
 
-def _masks(T, topo, s, first, away):
+def _masks(T, topo, s, plan):
+    hi, lo, plain = plan[0], plan[1], plan[2]
     c = T.cores[s]
-    m_off = _common_mask(topo, c, [h for h, _r in away[s]])
-    m_on = _common_mask(topo, c, first[s])
-    if m_on & ~m_off:
-        m_on &= ~m_off
-    return m_on, m_off
+    m_lo = _common_mask(topo, c, lo[s] + [T.cores[d] for d in plain[s]])
+    m_hi = _common_mask(topo, c, hi[s]) & ~m_lo
+    return m_hi, m_lo
 
 
 def _relay_program(g, core, T, topo, plan):
-    first, away, role, when, by = plan
-    s, dests = role[core]
-    m_on, m_off = _masks(T, topo, s, first, away)
+    s, dests = plan[3][core]
+    m_hi, m_lo = _masks(T, topo, s, plan)
     sem = T.sem["a%d" % s]
-    g.wait_ge(sem, _count(m_on if core in first[s] else m_off))
+    g.wait_ge(sem, _count(m_hi if core in plan[0][s] else m_lo))
     dst = [T.cores[d] for d in dests]
     mask = _common_mask(topo, core, dst)
-    _send(g, T, topo, mask, T.relay[:, :], dst, [_slot(T, s) for _d in dests], sem)
+    g.remote_dma_fused([_transfer(topo, mask, T.relay[:, :], dst, [_slot(T, s) for _d in dests], sem)],
+                       local_sem=T.sem.loc)
     g.wait_ge(T.sem.loc, _count(mask))
 
 
 def _rank_program(g, core, T, topo, plan):
-    first, away, role, when, by = plan
+    hi, lo, plain, role, when, by = plan
     r = T.rank_of(core)
     S = T.sem
     v, t, sc, sy = g.vector, g.tensor, g.scalar, g.sync
@@ -152,21 +139,23 @@ def _rank_program(g, core, T, topo, plan):
     sc.dma_start(T.rms[0:N, :], T.rm[:, :]).then_inc(S.rm, 16)
     sy.dma_start(_slot(T, r), T.w[:, :]).then_inc(S.wo, 16)
 
-    g.iota(T.cmp[0:N, 0:N], [[1, N]], 0, -1, allow_small_or_imprecise_dtypes=True).then_inc(S.cm, 1)
-    m_on, m_off = _masks(T, topo, r, first, away)
+    g.iota(T.cmp[:, :], [[1, D]], 0, -1, allow_small_or_imprecise_dtypes=True).then_inc(S.cm, 1)
+    m_hi, m_lo = _masks(T, topo, r, plan)
     g.wait_ge(S.wd, 16)
     mine = S["a%d" % r]
-    _send(g, T, topo, m_on, T.wsrc[:, :], first[r], [T.relay[:, :] for _h in first[r]], mine)
-    _send(g, T, topo, m_off, T.wsrc[:, :], [h for h, _x in away[r]],
-          [T.relay[:, :] if x else _slot(T, r) for _h, x in away[r]], mine)
-    g.wait_ge(S.loc, _count(m_on) + _count(m_off))
+    g.remote_dma_fused([_transfer(topo, m_hi, T.wsrc[:, :], hi[r], [T.relay[:, :] for _h in hi[r]], mine),
+                        _transfer(topo, m_lo, T.wsrc[:, :], lo[r], [T.relay[:, :] for _h in lo[r]], mine)],
+                       local_sem=S.loc)
+    g.remote_dma_fused([_transfer(topo, m_lo, T.wsrc[:, :], [T.cores[d] for d in plain[r]],
+                                  [_slot(T, r) for _d in plain[r]], mine)], local_sem=S.loc)
+    g.wait_ge(S.loc, _count(m_hi) + 2 * _count(m_lo))
 
-    v.memset(T.ones[0:N, :], 1.0).then_inc(S.pre, 1)
+    v.memset(T.ones[:, :], 1.0).then_inc(S.pre, 1)
     v.wait_ge(S.cm, 1)
-    v.tensor_scalar(T.i9[0:N, 0:N], T.cmp[0:N, 0:N], 0.0, None, AluOpType.is_equal).then_inc(S.pre, 1)
+    v.tensor_scalar(T.eye[:, :], T.cmp[:, :], 0.0, None, AluOpType.is_equal).then_inc(S.pre, 1)
     v.wait_ge(S.pre, 2)
     for i, e in enumerate(order):
-        v.tensor_scalar(T.sel[0:N, i * D:(i + 1) * D], T.ones[0:N, :], T.i9[0:N, e:e + 1], None, mult).then_inc(S.sel, 1)
+        v.tensor_scalar(T.sel[0:N, i * D:(i + 1) * D], T.ones[0:N, :], T.eye[0:N, e:e + 1], None, mult).then_inc(S.sel, 1)
 
     t.wait_ge(S.xr, 32)
     t.matmul(T.ps_sc[0:N, 0:D], T.rts[:, 0:N], T.xs[:, :], True, True).then_inc(S.sc, 1)
@@ -179,6 +168,14 @@ def _rank_program(g, core, T, topo, plan):
     t.wait_ge(S.pre, 2)
     t.wait_ge(S.sel, N)
     t.wait_ge(S.am, 1)
+    t.matmul(T.ps_sc[:, 3 * D:3 * D + 1], T.am[0:N, :], T.ones[0:N, 0:1], True, True).then_inc(S.dt, 1)
+    v.wait_ge(S.dt, 1)
+    v.tensor_scalar(T.dn[:, 0:1], T.ps_sc[:, 3 * D:3 * D + 1], EPS, None, AluOpType.add).then_inc(S.dn, 1)
+    v.wait_ge(S.dn, 1)
+    v.reciprocal(T.rd[:, 0:1], T.dn[:, 0:1]).then_inc(S.rd, 1)
+    v.wait_ge(S.rd, 1)
+    v.tensor_scalar(T.dg[:, :], T.eye[:, :], T.rd[:, 0:1], None, mult).then_inc(S.dg, 1)
+
     v.wait_ge(S.xr, 32)
     for j, grp in enumerate(groups):
         for i in grp:
@@ -187,11 +184,10 @@ def _rank_program(g, core, T, topo, plan):
         v.wait_ge(S["b%d" % j], len(grp))
         for i in grp:
             v.tensor_tensor(blk(T.xg, i), blk(T["pb%d" % j], i - grp[0]), T.xs[:, :], mult).then_inc(S["x%d" % j], 1)
-    t.matmul(T.ps_sc[:, 2 * D:3 * D], T.ones[0:N, :], T.am[0:N, :], True, True).then_inc(S.den, 1)
-    sc.wait_ge(S.den, 1)
-    sc.activation(T.r0[:, :], T.ps_sc[:, 2 * D:3 * D], ActivationFunctionType.Identity, bias=EPS).then_inc(S.r0, 1)
-    v.wait_ge(S.r0, 1)
-    v.reciprocal(T.rr[:, :], T.r0[:, :]).then_inc(S.rr, 1)
+    t.wait_ge(S.dg, 1)
+    t.matmul(T.ps_sc[:, 2 * D:3 * D], T.ones[:, :], T.dg[:, :], True, True).then_inc(S.rp, 1)
+    sc.wait_ge(S.rp, 1)
+    sc.activation(T.rr[:, :], T.ps_sc[:, 2 * D:3 * D], ActivationFunctionType.Copy).then_inc(S.rr, 1)
 
     for i, e in enumerate(order):
         if i % GROUP == 0:
@@ -201,7 +197,7 @@ def _rank_program(g, core, T, topo, plan):
         else:
             h = by[r][e]
             if h == T.cores[e]:
-                cnt = _count(_masks(T, topo, e, first, away)[1])
+                cnt = _count(_masks(T, topo, e, plan)[1])
             else:
                 cnt = _count(_common_mask(topo, h, [T.cores[d] for d in role[h][1]]))
             t.wait_ge(S["a%d" % e], cnt)
@@ -219,5 +215,5 @@ def rank_program(g, core, T, topo):
     plan = _plan(T, topo)
     if T.rank_of(core) is not None:
         _rank_program(g, core, T, topo, plan)
-    elif core in plan[2]:
+    elif core in plan[3]:
         _relay_program(g, core, T, topo, plan)

@@ -17,6 +17,7 @@ SCRATCH = {
     "rms": ("sbuf", [128, D], "bfloat16"),
     "cmp": ("sbuf", [128, D], "float32"),
     "eye": ("sbuf", [128, D], "bfloat16"),
+    "e9": ("sbuf", [128, 16], "bfloat16"),
     "ones": ("sbuf", [128, D], "bfloat16"),
     "sel": ("sbuf", [128, N * D], "bfloat16"),
     "am": ("sbuf", [128, D], "bfloat16"),
@@ -32,8 +33,8 @@ SCRATCH = {
 for _j in range(NB):
     SCRATCH["pb%d" % _j] = ("psum", [128, 512], "float32")
 
-SEMAPHORES = (["wd", "wo", "xr", "rm", "cm", "pre", "sel", "sc", "a", "am", "dt", "dn", "rd", "dg", "rp", "rr", "mm",
-               "y", "st", "loc"]
+SEMAPHORES = (["wd", "wo", "xr", "rm", "cm", "pre", "ey", "sel", "sc", "a", "am", "dt", "dn", "rd", "dg", "rp", "rr",
+               "mm", "y", "st", "loc"]
               + ["b%d" % j for j in range(NB)] + ["x%d" % j for j in range(NB)] + ["a%d" % s for s in range(N)])
 
 
@@ -109,16 +110,31 @@ def _masks(T, topo, s, plan):
     return m_hi, m_lo
 
 
+def _relay_mask(T, topo, h, plan):
+    s, dests = plan[3][h]
+    return _common_mask(topo, h, [T.cores[d] for d in dests] + [T.cores[s]])
+
+
 def _relay_program(g, core, T, topo, plan):
     s, dests = plan[3][core]
+    S = T.sem
     m_hi, m_lo = _masks(T, topo, s, plan)
-    sem = T.sem["a%d" % s]
+    team = plan[0][s] + plan[1][s]
+    q = team.index(core)
+    c0, c1 = D * q // len(team), D * (q + 1) // len(team)
+    wd = c1 - c0
+    mask = _relay_mask(T, topo, core, plan)
+    g.iota(T.cmp[:, 0:wd], [[1, wd]], c0, -1, allow_small_or_imprecise_dtypes=True).then_inc(S.cm, 1)
+    g.vector.wait_ge(S.cm, 1)
+    g.vector.tensor_scalar(T.eye[:, 0:wd], T.cmp[:, 0:wd], 0.0, None, AluOpType.is_equal).then_inc(S.pre, 1)
+    g.wait_ge(S.pre, 1)
+    g.remote_dma_fused([_transfer(topo, mask, T.eye[:, 0:wd], [T.cores[s]], [T.eye[:, c0:c1]], S.ey)], local_sem=S.loc)
+    sem = S["a%d" % s]
     g.wait_ge(sem, _count(m_hi if core in plan[0][s] else m_lo))
     dst = [T.cores[d] for d in dests]
-    mask = _common_mask(topo, core, dst)
     g.remote_dma_fused([_transfer(topo, mask, T.relay[:, :], dst, [_slot(T, s) for _d in dests], sem)],
-                       local_sem=T.sem.loc)
-    g.wait_ge(T.sem.loc, _count(mask))
+                       local_sem=S.loc)
+    g.wait_ge(S.loc, 2 * _count(mask))
 
 
 def _rank_program(g, core, T, topo, plan):
@@ -128,6 +144,7 @@ def _rank_program(g, core, T, topo, plan):
     v, t, sc, sy = g.vector, g.tensor, g.scalar, g.sync
     mult = AluOpType.mult
     order = [r] + sorted(when[r], key=lambda s: (when[r][s], s))
+    early = 1 + len([s for s in when[r] if by[r][s] == T.cores[s]])
     groups = [list(range(j * GROUP, min(N, (j + 1) * GROUP))) for j in range(NB)]
 
     def blk(buf, i):
@@ -139,7 +156,7 @@ def _rank_program(g, core, T, topo, plan):
     sc.dma_start(T.rms[0:N, :], T.rm[:, :]).then_inc(S.rm, 16)
     sy.dma_start(_slot(T, r), T.w[:, :]).then_inc(S.wo, 16)
 
-    g.iota(T.cmp[:, :], [[1, D]], 0, -1, allow_small_or_imprecise_dtypes=True).then_inc(S.cm, 1)
+    g.iota(T.cmp[0:N, 0:16], [[1, 16]], 0, -1, allow_small_or_imprecise_dtypes=True).then_inc(S.cm, 1)
     m_hi, m_lo = _masks(T, topo, r, plan)
     g.wait_ge(S.wd, 16)
     mine = S["a%d" % r]
@@ -152,10 +169,10 @@ def _rank_program(g, core, T, topo, plan):
 
     v.memset(T.ones[:, :], 1.0).then_inc(S.pre, 1)
     v.wait_ge(S.cm, 1)
-    v.tensor_scalar(T.eye[:, :], T.cmp[:, :], 0.0, None, AluOpType.is_equal).then_inc(S.pre, 1)
+    v.tensor_scalar(T.e9[0:N, 0:16], T.cmp[0:N, 0:16], 0.0, None, AluOpType.is_equal).then_inc(S.pre, 1)
     v.wait_ge(S.pre, 2)
     for i, e in enumerate(order):
-        v.tensor_scalar(T.sel[0:N, i * D:(i + 1) * D], T.ones[0:N, :], T.eye[0:N, e:e + 1], None, mult).then_inc(S.sel, 1)
+        v.tensor_scalar(T.sel[0:N, i * D:(i + 1) * D], T.ones[0:N, :], T.e9[0:N, e:e + 1], None, mult).then_inc(S.sel, 1)
 
     t.wait_ge(S.xr, 32)
     t.matmul(T.ps_sc[0:N, 0:D], T.rts[:, 0:N], T.xs[:, :], True, True).then_inc(S.sc, 1)
@@ -169,12 +186,8 @@ def _rank_program(g, core, T, topo, plan):
     t.wait_ge(S.sel, N)
     t.wait_ge(S.am, 1)
     t.matmul(T.ps_sc[:, 3 * D:3 * D + 1], T.am[0:N, :], T.ones[0:N, 0:1], True, True).then_inc(S.dt, 1)
-    v.wait_ge(S.dt, 1)
-    v.tensor_scalar(T.dn[:, 0:1], T.ps_sc[:, 3 * D:3 * D + 1], EPS, None, AluOpType.add).then_inc(S.dn, 1)
-    v.wait_ge(S.dn, 1)
-    v.reciprocal(T.rd[:, 0:1], T.dn[:, 0:1]).then_inc(S.rd, 1)
-    v.wait_ge(S.rd, 1)
-    v.tensor_scalar(T.dg[:, :], T.eye[:, :], T.rd[:, 0:1], None, mult).then_inc(S.dg, 1)
+    sc.wait_ge(S.dt, 1)
+    sc.activation(T.dn[:, 0:1], T.ps_sc[:, 3 * D:3 * D + 1], ActivationFunctionType.Identity, bias=EPS).then_inc(S.dn, 1)
 
     v.wait_ge(S.xr, 32)
     for j, grp in enumerate(groups):
@@ -184,12 +197,17 @@ def _rank_program(g, core, T, topo, plan):
         v.wait_ge(S["b%d" % j], len(grp))
         for i in grp:
             v.tensor_tensor(blk(T.xg, i), blk(T["pb%d" % j], i - grp[0]), T.xs[:, :], mult).then_inc(S["x%d" % j], 1)
-    t.wait_ge(S.dg, 1)
-    t.matmul(T.ps_sc[:, 2 * D:3 * D], T.ones[:, :], T.dg[:, :], True, True).then_inc(S.rp, 1)
-    sc.wait_ge(S.rp, 1)
-    sc.activation(T.rr[:, :], T.ps_sc[:, 2 * D:3 * D], ActivationFunctionType.Copy).then_inc(S.rr, 1)
+        if j == 0:
+            v.wait_ge(S.dn, 1)
+            v.reciprocal(T.rd[:, 0:1], T.dn[:, 0:1]).then_inc(S.rd, 1)
+    sc.wait_ge(S.rd, 1)
+    sc.wait_ge(S.ey, sum(_count(_relay_mask(T, topo, h, plan)) for h in hi[r] + lo[r]))
+    sc.activation(T.dg[:, :], T.eye[:, :], ActivationFunctionType.Copy, scale=T.rd[:, 0:1]).then_inc(S.dg, 1)
 
     for i, e in enumerate(order):
+        if i == early:
+            t.wait_ge(S.dg, 1)
+            t.matmul(T.ps_sc[:, 2 * D:3 * D], T.ones[:, :], T.dg[:, :], True, True).then_inc(S.rp, 1)
         if i % GROUP == 0:
             t.wait_ge(S["x%d" % (i // GROUP)], len(groups[i // GROUP]))
         if e == r:
@@ -199,9 +217,11 @@ def _rank_program(g, core, T, topo, plan):
             if h == T.cores[e]:
                 cnt = _count(_masks(T, topo, e, plan)[1])
             else:
-                cnt = _count(_common_mask(topo, h, [T.cores[d] for d in role[h][1]]))
+                cnt = _count(_relay_mask(T, topo, h, plan))
             t.wait_ge(S["a%d" % e], cnt)
         t.matmul(T.ps_acc[:, 0:D], _slot(T, e), blk(T.xg, i), i == 0, i == N - 1).then_inc(S.mm, 1)
+    sc.wait_ge(S.rp, 1)
+    sc.activation(T.rr[:, :], T.ps_sc[:, 2 * D:3 * D], ActivationFunctionType.Copy).then_inc(S.rr, 1)
 
     v.wait_ge(S.rr, 1)
     v.wait_ge(S.mm, N)

@@ -3,7 +3,10 @@ from concourse.mybir import AluOpType, ActivationFunctionType
 
 N = 9
 D = 128
+H = D // 2
 EPS = 0.01
+OFF = 1e28
+CW = 26
 SIM_CORES = 96
 GROUP = 2
 NB = (N + GROUP - 1) // GROUP
@@ -15,10 +18,14 @@ SCRATCH = {
     "xs": ("sbuf", [128, D], "bfloat16"),
     "rts": ("sbuf", [128, 16], "bfloat16"),
     "rms": ("sbuf", [128, D], "bfloat16"),
+    "ngm": ("sbuf", [128, D], "bfloat16"),
     "cmp": ("sbuf", [128, D], "float32"),
+    "cb": ("sbuf", [128, 32], "bfloat16"),
     "eye": ("sbuf", [128, D], "bfloat16"),
     "e9": ("sbuf", [128, 16], "bfloat16"),
+    "hun": ("sbuf", [128, D], "bfloat16"),
     "ones": ("sbuf", [128, D], "bfloat16"),
+    "vone": ("sbuf", [128, D], "bfloat16"),
     "sel": ("sbuf", [128, N * D], "bfloat16"),
     "am": ("sbuf", [128, D], "bfloat16"),
     "xg": ("sbuf", [128, N * D], "bfloat16"),
@@ -28,13 +35,14 @@ SCRATCH = {
     "rr": ("sbuf", [128, D], "float32"),
     "ysb": ("sbuf", [128, D], "bfloat16"),
     "ps_sc": ("psum", [128, 512], "float32"),
-    "ps_acc": ("psum", [128, 512], "float32"),
+    "ps_a": ("psum", [128, 512], "float32"),
+    "ps_b": ("psum", [128, 512], "float32"),
 }
 for _j in range(NB):
     SCRATCH["pb%d" % _j] = ("psum", [128, 512], "float32")
 
-SEMAPHORES = (["wd", "wo", "xr", "rm", "cm", "pre", "ey", "sel", "sc", "a", "am", "dt", "dn", "rd", "dg", "rp", "rr",
-               "mm", "y", "st", "loc"]
+SEMAPHORES = (["wd", "wo", "xr", "rm", "cm", "hc", "pre", "ey", "sel", "sc", "h", "on", "nm", "am", "dt", "dn", "rd",
+               "dg", "rp", "rr", "ma", "mb", "y", "st", "loc"]
               + ["b%d" % j for j in range(NB)] + ["x%d" % j for j in range(NB)] + ["a%d" % s for s in range(N)])
 
 
@@ -52,7 +60,7 @@ def _common_mask(topo, src, dsts):
 def _plan(T, topo):
     cores = list(T.cores)
     n = len(cores)
-    hi, lo, plain, role = {}, {}, {}, {}
+    hi, lo, plain, role, fifth = {}, {}, {}, {}, {}
     when = {r: {} for r in range(n)}
     by = {r: {} for r in range(n)}
     met = {}
@@ -62,6 +70,8 @@ def _plan(T, topo):
         cross = [d for d in ring if not topo.may_write(c, cores[d])]
         owners = [h for h in range(SIM_CORES) if topo.chip(h) == topo.chip(c) and h not in cores
                   and all(topo.may_write(h, cores[d]) for d in cross)]
+        fifth[s] = [h for h in range(SIM_CORES) if topo.chip(h) == topo.chip(c) and h not in cores
+                    and h not in owners and topo.die(h) == topo.die(c)][0]
         near = [h for h in owners if topo.die(h) == topo.die(c)]
         far = [h for h in owners if topo.die(h) != topo.die(c)]
         mate = [d for d in cross if topo.mates(topo.chip(c), topo.chip(cores[d]))]
@@ -87,7 +97,7 @@ def _plan(T, topo):
         for i, d in enumerate(plain[s]):
             when[d][s] = 1.0 + 0.1 * i
             by[d][s] = c
-    return hi, lo, plain, role, when, by
+    return hi, lo, plain, role, when, by, fifth
 
 
 def _slot(T, e):
@@ -115,13 +125,17 @@ def _relay_mask(T, topo, h, plan):
     return _common_mask(topo, h, [T.cores[d] for d in dests] + [T.cores[s]])
 
 
+def _block(plan, s, core):
+    team = plan[0][s] + plan[1][s] + [plan[6][s]]
+    q = team.index(core)
+    return D * q // len(team), D * (q + 1) // len(team)
+
+
 def _relay_program(g, core, T, topo, plan):
     s, dests = plan[3][core]
     S = T.sem
     m_hi, m_lo = _masks(T, topo, s, plan)
-    team = plan[0][s] + plan[1][s]
-    q = team.index(core)
-    c0, c1 = D * q // len(team), D * (q + 1) // len(team)
+    c0, c1 = _block(plan, s, core)
     wd = c1 - c0
     mask = _relay_mask(T, topo, core, plan)
     g.iota(T.cmp[:, 0:wd], [[1, wd]], c0, -1, allow_small_or_imprecise_dtypes=True).then_inc(S.cm, 1)
@@ -137,8 +151,20 @@ def _relay_program(g, core, T, topo, plan):
     g.wait_ge(S.loc, 2 * _count(mask))
 
 
+def _fifth_program(g, core, T, topo, plan, s):
+    S = T.sem
+    c0, c1 = _block(plan, s, core)
+    wd = c1 - c0
+    back = topo.mask(core, T.cores[s])
+    g.vector.wait_ge(S.hc, _count(topo.mask(T.cores[s], core)))
+    g.vector.tensor_scalar(T.eye[:, 0:wd], T.cb[:, 0:wd], float(-c0), None, AluOpType.is_equal).then_inc(S.pre, 1)
+    g.wait_ge(S.pre, 1)
+    g.remote_dma_fused([_transfer(topo, back, T.eye[:, 0:wd], [T.cores[s]], [T.eye[:, c0:c1]], S.ey)], local_sem=S.loc)
+    g.wait_ge(S.loc, _count(back))
+
+
 def _rank_program(g, core, T, topo, plan):
-    hi, lo, plain, role, when, by = plan
+    hi, lo, plain, role, when, by, fifth = plan
     r = T.rank_of(core)
     S = T.sem
     v, t, sc, sy = g.vector, g.tensor, g.scalar, g.sync
@@ -152,11 +178,14 @@ def _rank_program(g, core, T, topo, plan):
 
     sy.dma_start(T.wsrc[:, :], T.w[:, :]).then_inc(S.wd, 16)
     sc.dma_start(T.xs[:, :], T.x[:, :]).then_inc(S.xr, 16)
-    sy.dma_start(T.rts[:, 0:N], T.rt[:, :]).then_inc(S.xr, 16)
-    sc.dma_start(T.rms[0:N, :], T.rm[:, :]).then_inc(S.rm, 16)
+    sy.dma_start(T.rms[0:N, :], T.rm[:, :]).then_inc(S.rm, 16)
+    sc.dma_start(T.rts[:, 0:N], T.rt[:, :]).then_inc(S.xr, 16)
     sy.dma_start(_slot(T, r), T.w[:, :]).then_inc(S.wo, 16)
 
-    g.iota(T.cmp[0:N, 0:16], [[1, 16]], 0, -1, allow_small_or_imprecise_dtypes=True).then_inc(S.cm, 1)
+    g.iota(T.cb[:, 0:CW], [[1, CW]], 0, -1, allow_small_or_imprecise_dtypes=True).then_inc(S.cm, 1)
+    g.wait_ge(S.cm, 1)
+    m_5 = topo.mask(core, fifth[r])
+    g.remote_dma_fused([_transfer(topo, m_5, T.cb[:, 0:CW], [fifth[r]], [T.cb[:, 0:CW]], S.hc)], local_sem=S.loc)
     m_hi, m_lo = _masks(T, topo, r, plan)
     g.wait_ge(S.wd, 16)
     mine = S["a%d" % r]
@@ -165,43 +194,50 @@ def _rank_program(g, core, T, topo, plan):
                        local_sem=S.loc)
     g.remote_dma_fused([_transfer(topo, m_lo, T.wsrc[:, :], [T.cores[d] for d in plain[r]],
                                   [_slot(T, r) for _d in plain[r]], mine)], local_sem=S.loc)
-    g.wait_ge(S.loc, _count(m_hi) + 2 * _count(m_lo))
+    g.wait_ge(S.loc, _count(m_5) + _count(m_hi) + 2 * _count(m_lo))
 
-    v.memset(T.ones[:, :], 1.0).then_inc(S.pre, 1)
+    v.memset(T.hun[:, :], 100.0).then_inc(S.h, 1)
+    v.memset(T.vone[0:N, :], 1.0).then_inc(S.pre, 1)
     v.wait_ge(S.cm, 1)
-    v.tensor_scalar(T.e9[0:N, 0:16], T.cmp[0:N, 0:16], 0.0, None, AluOpType.is_equal).then_inc(S.pre, 1)
+    v.tensor_scalar(T.e9[0:N, 0:16], T.cb[0:N, 0:16], 0.0, None, AluOpType.is_equal).then_inc(S.pre, 1)
     v.wait_ge(S.pre, 2)
     for i, e in enumerate(order):
-        v.tensor_scalar(T.sel[0:N, i * D:(i + 1) * D], T.ones[0:N, :], T.e9[0:N, e:e + 1], None, mult).then_inc(S.sel, 1)
-
-    t.wait_ge(S.xr, 32)
-    t.matmul(T.ps_sc[0:N, 0:D], T.rts[:, 0:N], T.xs[:, :], True, True).then_inc(S.sc, 1)
-    sc.wait_ge(S.sc, 1)
-    sc.activation(T.ps_sc[0:N, D:2 * D], T.ps_sc[0:N, 0:D], ActivationFunctionType.Sigmoid).then_inc(S.a, 1)
-    v.wait_ge(S.a, 1)
+        v.tensor_scalar(T.sel[0:N, i * D:(i + 1) * D], T.vone[0:N, :], T.e9[0:N, e:e + 1], None, mult).then_inc(S.sel, 1)
     v.wait_ge(S.rm, 16)
-    v.tensor_tensor(T.am[0:N, :], T.ps_sc[0:N, D:2 * D], T.rms[0:N, :], mult).then_inc(S.am, 1)
+    v.tensor_scalar(T.ngm[0:N, :], T.rms[0:N, :], 1.0, OFF, AluOpType.subtract, mult).then_inc(S.nm, 1)
+
+    sc.wait_ge(S.h, 1)
+    sc.activation(T.ones[:, :], T.hun[:, :], ActivationFunctionType.Sigmoid).then_inc(S.on, 1)
 
     t.wait_ge(S.pre, 2)
+    t.wait_ge(S.nm, 1)
+    t.matmul(T.ps_sc[0:N, 0:D], T.e9[0:N, 0:N], T.ngm[0:N, :], True, False)
+    t.wait_ge(S.xr, 32)
+    t.matmul(T.ps_sc[0:N, 0:D], T.rts[:, 0:N], T.xs[:, :], False, True).then_inc(S.sc, 1)
+    sc.wait_ge(S.sc, 1)
+    sc.activation(T.am[0:N, :], T.ps_sc[0:N, 0:D], ActivationFunctionType.Sigmoid).then_inc(S.am, 1)
+
     t.wait_ge(S.sel, N)
     t.wait_ge(S.am, 1)
-    t.matmul(T.ps_sc[:, 3 * D:3 * D + 1], T.am[0:N, :], T.ones[0:N, 0:1], True, True).then_inc(S.dt, 1)
-    sc.wait_ge(S.dt, 1)
-    sc.activation(T.dn[:, 0:1], T.ps_sc[:, 3 * D:3 * D + 1], ActivationFunctionType.Identity, bias=EPS).then_inc(S.dn, 1)
-
     v.wait_ge(S.xr, 32)
     for j, grp in enumerate(groups):
         for i in grp:
             t.matmul(blk(T["pb%d" % j], i - grp[0]), T.sel[0:N, i * D:(i + 1) * D], T.am[0:N, :], True, True) \
                 .then_inc(S["b%d" % j], 1)
+        if j == 0:
+            t.wait_ge(S.on, 1)
+            t.matmul(T.ps_sc[:, 3 * D:3 * D + 1], T.am[0:N, :], T.ones[0:N, 0:1], True, True).then_inc(S.dt, 1)
+            sc.wait_ge(S.dt, 1)
+            sc.activation(T.dn[:, 0:1], T.ps_sc[:, 3 * D:3 * D + 1], ActivationFunctionType.Identity, bias=EPS) \
+                .then_inc(S.dn, 1)
         v.wait_ge(S["b%d" % j], len(grp))
         for i in grp:
             v.tensor_tensor(blk(T.xg, i), blk(T["pb%d" % j], i - grp[0]), T.xs[:, :], mult).then_inc(S["x%d" % j], 1)
-        if j == 0:
+        if j == 1:
             v.wait_ge(S.dn, 1)
             v.reciprocal(T.rd[:, 0:1], T.dn[:, 0:1]).then_inc(S.rd, 1)
     sc.wait_ge(S.rd, 1)
-    sc.wait_ge(S.ey, sum(_count(_relay_mask(T, topo, h, plan)) for h in hi[r] + lo[r]))
+    sc.wait_ge(S.ey, sum(_count(_relay_mask(T, topo, h, plan)) for h in hi[r] + lo[r]) + _count(topo.mask(fifth[r], core)))
     sc.activation(T.dg[:, :], T.eye[:, :], ActivationFunctionType.Copy, scale=T.rd[:, 0:1]).then_inc(S.dg, 1)
 
     for i, e in enumerate(order):
@@ -219,14 +255,17 @@ def _rank_program(g, core, T, topo, plan):
             else:
                 cnt = _count(_relay_mask(T, topo, h, plan))
             t.wait_ge(S["a%d" % e], cnt)
-        t.matmul(T.ps_acc[:, 0:D], _slot(T, e), blk(T.xg, i), i == 0, i == N - 1).then_inc(S.mm, 1)
+        t.matmul(T.ps_a[:, 0:H], _slot(T, e), T.xg[:, i * D:i * D + H], i == 0, i == N - 1).then_inc(S.ma, 1)
+        t.matmul(T.ps_b[:, 0:H], _slot(T, e), T.xg[:, i * D + H:(i + 1) * D], i == 0, i == N - 1).then_inc(S.mb, 1)
     sc.wait_ge(S.rp, 1)
     sc.activation(T.rr[:, :], T.ps_sc[:, 2 * D:3 * D], ActivationFunctionType.Copy).then_inc(S.rr, 1)
 
     v.wait_ge(S.rr, 1)
-    v.wait_ge(S.mm, N)
-    v.tensor_tensor(T.ysb[:, :], T.ps_acc[:, 0:D], T.rr[:, :], mult).then_inc(S.y, 1)
-    sy.wait_ge(S.y, 1)
+    v.wait_ge(S.ma, N)
+    v.tensor_tensor(T.ysb[:, 0:H], T.ps_a[:, 0:H], T.rr[:, 0:H], mult).then_inc(S.y, 1)
+    v.wait_ge(S.mb, N)
+    v.tensor_tensor(T.ysb[:, H:D], T.ps_b[:, 0:H], T.rr[:, H:D], mult).then_inc(S.y, 1)
+    sy.wait_ge(S.y, 2)
     sy.dma_start(T.y[:, :], T.ysb[:, :]).then_inc(S.st, 16)
     sy.wait_ge(S.st, 16)
 
@@ -237,3 +276,7 @@ def rank_program(g, core, T, topo):
         _rank_program(g, core, T, topo, plan)
     elif core in plan[3]:
         _relay_program(g, core, T, topo, plan)
+    else:
+        for s in plan[6]:
+            if plan[6][s] == core:
+                _fifth_program(g, core, T, topo, plan, s)

from concourse.bass import DstId, RemoteDMATransfer
from concourse.mybir import AluOpType, ActivationFunctionType

N = 9
D = 128
H = D // 2
EPS = 0.01
OFF = 1e28
CW = 26
SIM_CORES = 96
GROUP = 2
NB = (N + GROUP - 1) // GROUP

SCRATCH = {
    "wsrc": ("dram", [128, D], "bfloat16"),
    "relay": ("dram", [128, D], "bfloat16"),
    "wall": ("sbuf", [128, N * D], "bfloat16"),
    "xs": ("sbuf", [128, D], "bfloat16"),
    "rts": ("sbuf", [128, 16], "bfloat16"),
    "rms": ("sbuf", [128, D], "bfloat16"),
    "ngm": ("sbuf", [128, D], "bfloat16"),
    "cmp": ("sbuf", [128, D], "float32"),
    "cb": ("sbuf", [128, 32], "bfloat16"),
    "eye": ("sbuf", [128, D], "bfloat16"),
    "e9": ("sbuf", [128, 16], "bfloat16"),
    "hun": ("sbuf", [128, D], "bfloat16"),
    "ones": ("sbuf", [128, D], "bfloat16"),
    "vone": ("sbuf", [128, D], "bfloat16"),
    "sel": ("sbuf", [128, N * D], "bfloat16"),
    "am": ("sbuf", [128, D], "bfloat16"),
    "xg": ("sbuf", [128, N * D], "bfloat16"),
    "dn": ("sbuf", [128, 4], "float32"),
    "rd": ("sbuf", [128, 4], "float32"),
    "dg": ("sbuf", [128, D], "bfloat16"),
    "rr": ("sbuf", [128, D], "float32"),
    "ysb": ("sbuf", [128, D], "bfloat16"),
    "ps_sc": ("psum", [128, 512], "float32"),
    "ps_a": ("psum", [128, 512], "float32"),
    "ps_b": ("psum", [128, 512], "float32"),
}
for _j in range(NB):
    SCRATCH["pb%d" % _j] = ("psum", [128, 512], "float32")

SEMAPHORES = (["wd", "wo", "xr", "rm", "cm", "hc", "pre", "ey", "sel", "sc", "h", "on", "nm", "am", "dt", "dn", "rd",
               "dg", "rp", "rr", "ma", "mb", "y", "st", "loc"]
              + ["b%d" % j for j in range(NB)] + ["x%d" % j for j in range(NB)] + ["a%d" % s for s in range(N)])


def _count(mask):
    return bin(mask).count("1")


def _common_mask(topo, src, dsts):
    m = topo.mask(src, dsts[0])
    for d in dsts[1:]:
        m &= topo.mask(src, d)
    return m


def _plan(T, topo):
    cores = list(T.cores)
    n = len(cores)
    hi, lo, plain, role, fifth = {}, {}, {}, {}, {}
    when = {r: {} for r in range(n)}
    by = {r: {} for r in range(n)}
    met = {}
    for s, c in enumerate(cores):
        ring = [(s + k) % n for k in range(1, n)]
        plain[s] = [d for d in ring if topo.may_write(c, cores[d])]
        cross = [d for d in ring if not topo.may_write(c, cores[d])]
        owners = [h for h in range(SIM_CORES) if topo.chip(h) == topo.chip(c) and h not in cores
                  and all(topo.may_write(h, cores[d]) for d in cross)]
        fifth[s] = [h for h in range(SIM_CORES) if topo.chip(h) == topo.chip(c) and h not in cores
                    and h not in owners and topo.die(h) == topo.die(c)][0]
        near = [h for h in owners if topo.die(h) == topo.die(c)]
        far = [h for h in owners if topo.die(h) != topo.die(c)]
        mate = [d for d in cross if topo.mates(topo.chip(c), topo.chip(cores[d]))]
        two = [d for d in cross if d not in mate]
        dn, df = topo.die(near[0]), topo.die(far[0])
        two.sort(key=lambda d: (met.get((d, dn), 0) - met.get((d, df), 0), ring.index(d)))
        k = len(two) - len(far)
        jobs = {h: [] for h in owners}
        for h, d in zip(far, two[k:]):
            jobs[h].append(d)
            met[(d, df)] = met.get((d, df), 0) + 1
        for i, d in enumerate(two[:k]):
            jobs[near[::-1][i % len(near)]].append(d)
            met[(d, dn)] = met.get((d, dn), 0) + 1
        jobs[near[0]] += mate
        hi[s] = [h for h in far if jobs[h]]
        lo[s] = [h for h in near[::-1] if jobs[h]]
        for h in hi[s] + lo[s]:
            role[h] = (s, jobs[h])
            for i, d in enumerate(jobs[h]):
                when[d][s] = 3.0 + i
                by[d][s] = h
        for i, d in enumerate(plain[s]):
            when[d][s] = 1.0 + 0.1 * i
            by[d][s] = c
    return hi, lo, plain, role, when, by, fifth


def _slot(T, e):
    return T.wall[:, e * D:(e + 1) * D]


def _transfer(topo, mask, src, dst_cores, dst_aps, sem):
    ids = []
    for d in dst_cores:
        rid, pid, _se = topo.addr(d)
        ids.append(DstId(rid=rid, pnc=pid))
    return RemoteDMATransfer(dst_ids=ids, dma_engine_mask=mask, remote_sem=sem, srcs=[src], dsts=dst_aps, alu_op=0)


def _masks(T, topo, s, plan):
    hi, lo, plain = plan[0], plan[1], plan[2]
    c = T.cores[s]
    m_lo = _common_mask(topo, c, lo[s] + [T.cores[d] for d in plain[s]])
    m_hi = _common_mask(topo, c, hi[s]) & ~m_lo
    return m_hi, m_lo


def _relay_mask(T, topo, h, plan):
    s, dests = plan[3][h]
    return _common_mask(topo, h, [T.cores[d] for d in dests] + [T.cores[s]])


def _block(plan, s, core):
    team = plan[0][s] + plan[1][s] + [plan[6][s]]
    q = team.index(core)
    return D * q // len(team), D * (q + 1) // len(team)


def _relay_program(g, core, T, topo, plan):
    s, dests = plan[3][core]
    S = T.sem
    m_hi, m_lo = _masks(T, topo, s, plan)
    c0, c1 = _block(plan, s, core)
    wd = c1 - c0
    mask = _relay_mask(T, topo, core, plan)
    g.iota(T.cmp[:, 0:wd], [[1, wd]], c0, -1, allow_small_or_imprecise_dtypes=True).then_inc(S.cm, 1)
    g.vector.wait_ge(S.cm, 1)
    g.vector.tensor_scalar(T.eye[:, 0:wd], T.cmp[:, 0:wd], 0.0, None, AluOpType.is_equal).then_inc(S.pre, 1)
    g.wait_ge(S.pre, 1)
    g.remote_dma_fused([_transfer(topo, mask, T.eye[:, 0:wd], [T.cores[s]], [T.eye[:, c0:c1]], S.ey)], local_sem=S.loc)
    sem = S["a%d" % s]
    g.wait_ge(sem, _count(m_hi if core in plan[0][s] else m_lo))
    dst = [T.cores[d] for d in dests]
    g.remote_dma_fused([_transfer(topo, mask, T.relay[:, :], dst, [_slot(T, s) for _d in dests], sem)],
                       local_sem=S.loc)
    g.wait_ge(S.loc, 2 * _count(mask))


def _fifth_program(g, core, T, topo, plan, s):
    S = T.sem
    c0, c1 = _block(plan, s, core)
    wd = c1 - c0
    back = topo.mask(core, T.cores[s])
    g.vector.wait_ge(S.hc, _count(topo.mask(T.cores[s], core)))
    g.vector.tensor_scalar(T.eye[:, 0:wd], T.cb[:, 0:wd], float(-c0), None, AluOpType.is_equal).then_inc(S.pre, 1)
    g.wait_ge(S.pre, 1)
    g.remote_dma_fused([_transfer(topo, back, T.eye[:, 0:wd], [T.cores[s]], [T.eye[:, c0:c1]], S.ey)], local_sem=S.loc)
    g.wait_ge(S.loc, _count(back))


def _rank_program(g, core, T, topo, plan):
    hi, lo, plain, role, when, by, fifth = plan
    r = T.rank_of(core)
    S = T.sem
    v, t, sc, sy = g.vector, g.tensor, g.scalar, g.sync
    mult = AluOpType.mult
    order = [r] + sorted(when[r], key=lambda s: (when[r][s], s))
    early = 1 + len([s for s in when[r] if by[r][s] == T.cores[s]])
    groups = [list(range(j * GROUP, min(N, (j + 1) * GROUP))) for j in range(NB)]

    def blk(buf, i):
        return buf[:, i * D:(i + 1) * D]

    sy.dma_start(T.wsrc[:, :], T.w[:, :]).then_inc(S.wd, 16)
    sc.dma_start(T.xs[:, :], T.x[:, :]).then_inc(S.xr, 16)
    sy.dma_start(T.rms[0:N, :], T.rm[:, :]).then_inc(S.rm, 16)
    sc.dma_start(T.rts[:, 0:N], T.rt[:, :]).then_inc(S.xr, 16)
    sy.dma_start(_slot(T, r), T.w[:, :]).then_inc(S.wo, 16)

    g.iota(T.cb[:, 0:CW], [[1, CW]], 0, -1, allow_small_or_imprecise_dtypes=True).then_inc(S.cm, 1)
    g.wait_ge(S.cm, 1)
    m_5 = topo.mask(core, fifth[r])
    g.remote_dma_fused([_transfer(topo, m_5, T.cb[:, 0:CW], [fifth[r]], [T.cb[:, 0:CW]], S.hc)], local_sem=S.loc)
    m_hi, m_lo = _masks(T, topo, r, plan)
    g.wait_ge(S.wd, 16)
    mine = S["a%d" % r]
    g.remote_dma_fused([_transfer(topo, m_hi, T.wsrc[:, :], hi[r], [T.relay[:, :] for _h in hi[r]], mine),
                        _transfer(topo, m_lo, T.wsrc[:, :], lo[r], [T.relay[:, :] for _h in lo[r]], mine)],
                       local_sem=S.loc)
    g.remote_dma_fused([_transfer(topo, m_lo, T.wsrc[:, :], [T.cores[d] for d in plain[r]],
                                  [_slot(T, r) for _d in plain[r]], mine)], local_sem=S.loc)
    g.wait_ge(S.loc, _count(m_5) + _count(m_hi) + 2 * _count(m_lo))

    v.memset(T.hun[:, :], 100.0).then_inc(S.h, 1)
    v.memset(T.vone[0:N, :], 1.0).then_inc(S.pre, 1)
    v.wait_ge(S.cm, 1)
    v.tensor_scalar(T.e9[0:N, 0:16], T.cb[0:N, 0:16], 0.0, None, AluOpType.is_equal).then_inc(S.pre, 1)
    v.wait_ge(S.pre, 2)
    for i, e in enumerate(order):
        v.tensor_scalar(T.sel[0:N, i * D:(i + 1) * D], T.vone[0:N, :], T.e9[0:N, e:e + 1], None, mult).then_inc(S.sel, 1)
    v.wait_ge(S.rm, 16)
    v.tensor_scalar(T.ngm[0:N, :], T.rms[0:N, :], 1.0, OFF, AluOpType.subtract, mult).then_inc(S.nm, 1)

    sc.wait_ge(S.h, 1)
    sc.activation(T.ones[:, :], T.hun[:, :], ActivationFunctionType.Sigmoid).then_inc(S.on, 1)

    t.wait_ge(S.pre, 2)
    t.wait_ge(S.nm, 1)
    t.matmul(T.ps_sc[0:N, 0:D], T.e9[0:N, 0:N], T.ngm[0:N, :], True, False)
    t.wait_ge(S.xr, 32)
    t.matmul(T.ps_sc[0:N, 0:D], T.rts[:, 0:N], T.xs[:, :], False, True).then_inc(S.sc, 1)
    sc.wait_ge(S.sc, 1)
    sc.activation(T.am[0:N, :], T.ps_sc[0:N, 0:D], ActivationFunctionType.Sigmoid).then_inc(S.am, 1)

    t.wait_ge(S.sel, N)
    t.wait_ge(S.am, 1)
    v.wait_ge(S.xr, 32)
    for j, grp in enumerate(groups):
        for i in grp:
            t.matmul(blk(T["pb%d" % j], i - grp[0]), T.sel[0:N, i * D:(i + 1) * D], T.am[0:N, :], True, True) \
                .then_inc(S["b%d" % j], 1)
        if j == 0:
            t.wait_ge(S.on, 1)
            t.matmul(T.ps_sc[:, 3 * D:3 * D + 1], T.am[0:N, :], T.ones[0:N, 0:1], True, True).then_inc(S.dt, 1)
            sc.wait_ge(S.dt, 1)
            sc.activation(T.dn[:, 0:1], T.ps_sc[:, 3 * D:3 * D + 1], ActivationFunctionType.Identity, bias=EPS) \
                .then_inc(S.dn, 1)
        v.wait_ge(S["b%d" % j], len(grp))
        for i in grp:
            v.tensor_tensor(blk(T.xg, i), blk(T["pb%d" % j], i - grp[0]), T.xs[:, :], mult).then_inc(S["x%d" % j], 1)
        if j == 1:
            v.wait_ge(S.dn, 1)
            v.reciprocal(T.rd[:, 0:1], T.dn[:, 0:1]).then_inc(S.rd, 1)
    sc.wait_ge(S.rd, 1)
    sc.wait_ge(S.ey, sum(_count(_relay_mask(T, topo, h, plan)) for h in hi[r] + lo[r]) + _count(topo.mask(fifth[r], core)))
    sc.activation(T.dg[:, :], T.eye[:, :], ActivationFunctionType.Copy, scale=T.rd[:, 0:1]).then_inc(S.dg, 1)

    for i, e in enumerate(order):
        if i == early:
            t.wait_ge(S.dg, 1)
            t.matmul(T.ps_sc[:, 2 * D:3 * D], T.ones[:, :], T.dg[:, :], True, True).then_inc(S.rp, 1)
        if i % GROUP == 0:
            t.wait_ge(S["x%d" % (i // GROUP)], len(groups[i // GROUP]))
        if e == r:
            t.wait_ge(S.wo, 16)
        else:
            h = by[r][e]
            if h == T.cores[e]:
                cnt = _count(_masks(T, topo, e, plan)[1])
            else:
                cnt = _count(_relay_mask(T, topo, h, plan))
            t.wait_ge(S["a%d" % e], cnt)
        t.matmul(T.ps_a[:, 0:H], _slot(T, e), T.xg[:, i * D:i * D + H], i == 0, i == N - 1).then_inc(S.ma, 1)
        t.matmul(T.ps_b[:, 0:H], _slot(T, e), T.xg[:, i * D + H:(i + 1) * D], i == 0, i == N - 1).then_inc(S.mb, 1)
    sc.wait_ge(S.rp, 1)
    sc.activation(T.rr[:, :], T.ps_sc[:, 2 * D:3 * D], ActivationFunctionType.Copy).then_inc(S.rr, 1)

    v.wait_ge(S.rr, 1)
    v.wait_ge(S.ma, N)
    v.tensor_tensor(T.ysb[:, 0:H], T.ps_a[:, 0:H], T.rr[:, 0:H], mult).then_inc(S.y, 1)
    v.wait_ge(S.mb, N)
    v.tensor_tensor(T.ysb[:, H:D], T.ps_b[:, 0:H], T.rr[:, H:D], mult).then_inc(S.y, 1)
    sy.wait_ge(S.y, 2)
    sy.dma_start(T.y[:, :], T.ysb[:, :]).then_inc(S.st, 16)
    sy.wait_ge(S.st, 16)


def rank_program(g, core, T, topo):
    plan = _plan(T, topo)
    if T.rank_of(core) is not None:
        _rank_program(g, core, T, topo, plan)
    elif core in plan[3]:
        _relay_program(g, core, T, topo, plan)
    else:
        for s in plan[6]:
            if plan[6][s] == core:
                _fifth_program(g, core, T, topo, plan, s)
